import numpy as np
CORES = [0,8,128,136,256,264,384,392]
N = 8
def setup_inputs(rng):
    return {"x1": rng.standard_normal((N, 128, 512), dtype=np.float32), "x2": rng.standard_normal((N, 128, 128), dtype=np.float32)}
def reference(x1, x2):
    out = []
    s = x1.sum(axis=0, dtype=np.float64).astype(x1.dtype)
    b = 512 // N
    out.append(np.stack([s[:, r * b:(r + 1) * b] for r in range(N)]))
    out.append(np.broadcast_to(x2[6], x2.shape))
    return {"y1": out[0], "y2": out[1]}

@@ -1,0 +1,117 @@
+from concourse.bass import DstId, RemoteDMATransfer
+
+SCRATCH = {
+    "xs": ("sbuf", [128, 512], "float32"),
+    "ina": ("sbuf", [128, 128], "float32"),
+    "inb": ("sbuf", [128, 128], "float32"),
+    "pc": ("sbuf", [128, 64], "float32"),
+    "pd": ("sbuf", [128, 64], "float32"),
+    "pm": ("sbuf", [128, 64], "float32"),
+    "r1": ("dram", [128, 64], "float32"),
+    "bc": ("dram", [128, 128], "float32"),
+}
+SEMAPHORES = ["ld1", "ld2", "st", "w1", "w2", "w3", "b1", "b2", "sent"]
+
+RELAY = [3, 2, 1, 0]
+X_CORE, MF_CORE, B_CORE = 2, 3, 6
+BC_FIRST = True
+
+
+def cid(h, p, k):
+    return 128 * h + 8 * p + k
+
+
+def rank_program(g, core, T, topo):
+    h, p, k = core // 128, (core % 128) // 8, core % 8
+    if p > 1:
+        return
+    S = T.sem
+
+    def to(d):
+        rid, pid = topo.addr(d, core)
+        return DstId(rid=rid, pnc=pid)
+
+    def blk(t, q):
+        return t[:, 64 * q:64 * q + 64]
+
+    root = T.cores[6]
+    rh, rp = root // 128, (root % 128) // 8
+    far = cid(3 - rh, rp, B_CORE)
+    near = cid(rh, rp, B_CORE)
+
+    if k == 0:
+        def send_x2():
+            g.wait_ge(S.ld2, 16)
+            g.remote_dma_fused([
+                RemoteDMATransfer(dst_ids=[to(far)], dma_engine_mask=0x00FF, remote_sem=S.b1, src=T.bc[:], dst=T.bc[:]),
+                RemoteDMATransfer(dst_ids=[to(near)], dma_engine_mask=0xFF00, remote_sem=S.b1, src=T.bc[:], dst=T.bc[:]),
+            ], local_sem=S.sent)
+
+        is_root = core == root
+        if is_root and BC_FIRST:
+            g.dma_start(out=T.bc[:], in_=T.x2[:]).then_inc(S.ld2, 16)
+        g.dma_start(out=T.xs[:], in_=T.x1[:]).then_inc(S.ld1, 16)
+        if is_root and not BC_FIRST:
+            g.dma_start(out=T.bc[:], in_=T.x2[:]).then_inc(S.ld2, 16)
+        if is_root and BC_FIRST:
+            send_x2()
+        g.wait_ge(S.ld1, 16)
+        off, on = [0x000F, 0x00F0], [0x0F00, 0xF000]
+        trs = []
+        for j in range(4):
+            src = T.xs[:, 128 * j:128 * j + 128]
+            if j == h:
+                d, buf, m = cid(h, p, MF_CORE), T.ina, on.pop()
+            elif RELAY[j] == h:
+                d, buf, m = cid(h, p, X_CORE), T.ina, on.pop()
+            elif j == h ^ 2:
+                d, buf, m = cid(RELAY[j], p, X_CORE), T.inb, off.pop()
+            else:
+                d, buf, m = cid(j, p, MF_CORE), T.inb, off.pop()
+            trs.append(RemoteDMATransfer(dst_ids=[to(d)], dma_engine_mask=m, remote_sem=S.w1, src=src, dst=buf[:]))
+        g.remote_dma_fused(trs, local_sem=S.sent)
+        if is_root:
+            if not BC_FIRST:
+                send_x2()
+            g.dma_start(out=T.y2[:], in_=T.x2[:]).then_inc(S.st, 16)
+        else:
+            g.wait_ge(S.b2, 8)
+            g.dma_start(out=T.y2[:], in_=T.bc[:]).then_inc(S.st, 16)
+        g.wait_ge(S.w3, 16)
+        g.dma_start(out=T.y1[:], in_=T.r1[:]).then_inc(S.st, 16)
+        g.wait_ge(S.sent, 32 if is_root else 16)
+        g.wait_ge(S.st, 32)
+
+    elif k == X_CORE:
+        j = RELAY.index(h)
+        g.wait_ge(S.w1, 8)
+        g.remote_dma_fused([
+            RemoteDMATransfer(dst_ids=[to(cid(j, q, MF_CORE))], dma_engine_mask=0x000F << (4 * q), remote_sem=S.w2,
+                              srcs=[blk(T.ina, q), blk(T.inb, q)], dsts=[(T.pc if q == p else T.pd)[:]], alu_op=1)
+            for q in range(2)], local_sem=S.sent)
+        g.wait_ge(S.sent, 8)
+
+    elif k == MF_CORE:
+        g.wait_ge(S.w1, 8)
+        g.remote_dma_fused([
+            RemoteDMATransfer(dst_ids=[to(cid(h, 1 - p, MF_CORE))], dma_engine_mask=0x00FF, remote_sem=S.w2,
+                              srcs=[blk(T.ina, 1 - p), blk(T.inb, 1 - p)], dsts=[T.pm[:]], alu_op=1)], local_sem=S.sent)
+        g.wait_ge(S.w2, 16)
+        g.remote_dma_fused([
+            RemoteDMATransfer(dst_ids=[to(cid(h, p, 0))], dma_engine_mask=0xFFFF, remote_sem=S.w3,
+                              srcs=[blk(T.ina, p), blk(T.inb, p), T.pc[:], T.pd[:], T.pm[:]], dsts=[T.r1[:]], alu_op=1)],
+            local_sem=S.sent)
+        g.wait_ge(S.sent, 24)
+
+    elif core in (far, near):
+        rack = [c for c in T.cores if topo.rack(topo.host(c)) == topo.rack(h) and c != root]
+        here = [c for c in rack if c // 8 == core // 8]
+        away = [c for c in rack if c // 8 != core // 8]
+        g.wait_ge(S.b1, 8)
+        trs = [RemoteDMATransfer(dst_ids=[to(c) for c in away], dma_engine_mask=0x00FF, remote_sem=S.b2,
+                                 srcs=[T.bc[:]], dsts=[T.bc[:] for c in away], alu_op=0)]
+        if here:
+            trs.append(RemoteDMATransfer(dst_ids=[to(here[0])], dma_engine_mask=0xFF00, remote_sem=S.b2,
+                                         src=T.bc[:], dst=T.bc[:]))
+        g.remote_dma_fused(trs, local_sem=S.sent)
+        g.wait_ge(S.sent, 8 * len(trs))

@@ -1,19 +1,21 @@
 from concourse.bass import DstId, RemoteDMATransfer
+from concourse.mybir import AluOpType
 
 SCRATCH = {
     "xs": ("sbuf", [128, 512], "float32"),
     "ina": ("sbuf", [128, 128], "float32"),
     "inb": ("sbuf", [128, 128], "float32"),
-    "pc": ("sbuf", [128, 64], "float32"),
-    "pd": ("sbuf", [128, 64], "float32"),
     "pm": ("sbuf", [128, 64], "float32"),
-    "r1": ("dram", [128, 64], "float32"),
+    "ma": ("sbuf", [128, 64], "float32"),
+    "mb": ("sbuf", [128, 64], "float32"),
+    "nb": ("dram", [128, 64], "float32"),
+    "n2": ("dram", [128, 64], "float32"),
+    "fp": ("dram", [128, 64], "float32"),
     "bc": ("dram", [128, 128], "float32"),
 }
-SEMAPHORES = ["ld1", "ld2", "st", "w1", "w2", "w3", "b1", "b2", "sent"]
+SEMAPHORES = ["ld1", "ld2", "st", "st2", "w1", "w2", "a1", "a2", "a3", "b1", "b2", "sent"]
 
-RELAY = [3, 2, 1, 0]
-X_CORE, MF_CORE, B_CORE = 2, 3, 6
+X_CORE, M_CORE, B_CORE = 2, 7, 6
 BC_FIRST = True
 
 
@@ -26,13 +28,18 @@ def rank_program(g, core, T, topo):
     if p > 1:
         return
     S = T.sem
+    s, c, q = h ^ 1, 3 - h, 1 - p
 
     def to(d):
         rid, pid = topo.addr(d, core)
         return DstId(rid=rid, pnc=pid)
 
-    def blk(t, q):
-        return t[:, 64 * q:64 * q + 64]
+    def blk(t, b):
+        return t[:, 64 * b:64 * b + 64]
+
+    def tr(d, mask, sem, srcs, dst):
+        return RemoteDMATransfer(dst_ids=[to(d)], dma_engine_mask=mask, remote_sem=sem, srcs=srcs, dsts=[dst],
+                                 alu_op=1 if len(srcs) > 1 else 0)
 
     root = T.cores[6]
     rh, rp = root // 128, (root % 128) // 8
@@ -42,10 +49,8 @@ def rank_program(g, core, T, topo):
     if k == 0:
         def send_x2():
             g.wait_ge(S.ld2, 16)
-            g.remote_dma_fused([
-                RemoteDMATransfer(dst_ids=[to(far)], dma_engine_mask=0x00FF, remote_sem=S.b1, src=T.bc[:], dst=T.bc[:]),
-                RemoteDMATransfer(dst_ids=[to(near)], dma_engine_mask=0xFF00, remote_sem=S.b1, src=T.bc[:], dst=T.bc[:]),
-            ], local_sem=S.sent)
+            g.remote_dma_fused([tr(far, 0x00FF, S.b1, [T.bc[:]], T.bc[:]), tr(near, 0xFF00, S.b1, [T.bc[:]], T.bc[:])],
+                               local_sem=S.sent)
 
         is_root = core == root
         if is_root and BC_FIRST:
@@ -56,62 +61,54 @@ def rank_program(g, core, T, topo):
         if is_root and BC_FIRST:
             send_x2()
         g.wait_ge(S.ld1, 16)
-        off, on = [0x000F, 0x00F0], [0x0F00, 0xF000]
-        trs = []
-        for j in range(4):
-            src = T.xs[:, 128 * j:128 * j + 128]
-            if j == h:
-                d, buf, m = cid(h, p, MF_CORE), T.ina, on.pop()
-            elif RELAY[j] == h:
-                d, buf, m = cid(h, p, X_CORE), T.ina, on.pop()
-            elif j == h ^ 2:
-                d, buf, m = cid(RELAY[j], p, X_CORE), T.inb, off.pop()
-            else:
-                d, buf, m = cid(j, p, MF_CORE), T.inb, off.pop()
-            trs.append(RemoteDMATransfer(dst_ids=[to(d)], dma_engine_mask=m, remote_sem=S.w1, src=src, dst=buf[:]))
-        g.remote_dma_fused(trs, local_sem=S.sent)
+        g.remote_dma_fused([
+            tr(cid(s, p, X_CORE), 0x00FF, S.w1, [T.xs[:, 128 * (h ^ 2):128 * (h ^ 2) + 128]], T.inb[:]),
+            tr(cid(h, p, X_CORE), 0xFF00, S.w1, [T.xs[:, 128 * c:128 * c + 128]], T.ina[:]),
+        ], local_sem=S.sent)
+        if is_root and not BC_FIRST:
+            send_x2()
+        g.remote_dma_fused([
+            tr(cid(s, p, 0), 0x000F, S.a1, [blk(T.xs, 2 * s + p)], T.nb[:]),
+            tr(cid(s, p, M_CORE), 0x00F0, S.w1, [blk(T.xs, 2 * s + q)], T.mb[:]),
+            tr(cid(h, p, M_CORE), 0xFF00, S.w1, [blk(T.xs, 2 * h + q)], T.ma[:]),
+        ], local_sem=S.sent)
+        g.dma_start(out=T.y1[:], in_=blk(T.x1, 2 * h + p)).then_inc(S.st, 16)
+        n = 16
+        for sem, cnt, buf in ((S.a1, 4, T.nb), (S.a2, 8, T.n2), (S.a3, 8, T.fp)):
+            g.wait_ge(sem, cnt)
+            g.wait_ge(S.st, n)
+            g.dma_start(out=T.y1[:], in_=buf[:], accum_op=AluOpType.add, max_dma_last_dim=8192).then_inc(S.st, 16)
+            n += 16
         if is_root:
-            if not BC_FIRST:
-                send_x2()
-            g.dma_start(out=T.y2[:], in_=T.x2[:]).then_inc(S.st, 16)
+            g.dma_start(out=T.y2[:], in_=T.x2[:]).then_inc(S.st2, 16)
         else:
             g.wait_ge(S.b2, 8)
-            g.dma_start(out=T.y2[:], in_=T.bc[:]).then_inc(S.st, 16)
-        g.wait_ge(S.w3, 16)
-        g.dma_start(out=T.y1[:], in_=T.r1[:]).then_inc(S.st, 16)
-        g.wait_ge(S.sent, 32 if is_root else 16)
-        g.wait_ge(S.st, 32)
+            g.dma_start(out=T.y2[:], in_=T.bc[:]).then_inc(S.st2, 16)
+        g.wait_ge(S.sent, 48 if is_root else 32)
+        g.wait_ge(S.st, n)
+        g.wait_ge(S.st2, 16)
 
     elif k == X_CORE:
-        j = RELAY.index(h)
-        g.wait_ge(S.w1, 8)
-        g.remote_dma_fused([
-            RemoteDMATransfer(dst_ids=[to(cid(j, q, MF_CORE))], dma_engine_mask=0x000F << (4 * q), remote_sem=S.w2,
-                              srcs=[blk(T.ina, q), blk(T.inb, q)], dsts=[(T.pc if q == p else T.pd)[:]], alu_op=1)
-            for q in range(2)], local_sem=S.sent)
+        g.wait_ge(S.w1, 16)
+        g.remote_dma_fused([tr(cid(h, q, X_CORE), 0x00FF, S.w2, [blk(T.ina, q), blk(T.inb, q)], T.pm[:])], local_sem=S.sent)
+        g.wait_ge(S.w2, 8)
+        g.remote_dma_fused([tr(cid(c, p, 0), 0x00FF, S.a3, [blk(T.ina, p), blk(T.inb, p), T.pm[:]], T.fp[:])],
+                           local_sem=S.sent)
+        g.wait_ge(S.sent, 16)
+
+    elif k == M_CORE:
+        g.wait_ge(S.w1, 12)
+        g.remote_dma_fused([tr(cid(h, q, 0), 0x00FF, S.a2, [T.ma[:], T.mb[:]], T.n2[:])], local_sem=S.sent)
         g.wait_ge(S.sent, 8)
 
-    elif k == MF_CORE:
-        g.wait_ge(S.w1, 8)
-        g.remote_dma_fused([
-            RemoteDMATransfer(dst_ids=[to(cid(h, 1 - p, MF_CORE))], dma_engine_mask=0x00FF, remote_sem=S.w2,
-                              srcs=[blk(T.ina, 1 - p), blk(T.inb, 1 - p)], dsts=[T.pm[:]], alu_op=1)], local_sem=S.sent)
-        g.wait_ge(S.w2, 16)
-        g.remote_dma_fused([
-            RemoteDMATransfer(dst_ids=[to(cid(h, p, 0))], dma_engine_mask=0xFFFF, remote_sem=S.w3,
-                              srcs=[blk(T.ina, p), blk(T.inb, p), T.pc[:], T.pd[:], T.pm[:]], dsts=[T.r1[:]], alu_op=1)],
-            local_sem=S.sent)
-        g.wait_ge(S.sent, 24)
-
     elif core in (far, near):
-        rack = [c for c in T.cores if topo.rack(topo.host(c)) == topo.rack(h) and c != root]
-        here = [c for c in rack if c // 8 == core // 8]
-        away = [c for c in rack if c // 8 != core // 8]
+        rack = [x for x in T.cores if topo.rack(topo.host(x)) == topo.rack(h) and x != root]
+        here = [x for x in rack if x // 8 == core // 8]
+        away = [x for x in rack if x // 8 != core // 8]
         g.wait_ge(S.b1, 8)
-        trs = [RemoteDMATransfer(dst_ids=[to(c) for c in away], dma_engine_mask=0x00FF, remote_sem=S.b2,
-                                 srcs=[T.bc[:]], dsts=[T.bc[:] for c in away], alu_op=0)]
+        trs = [RemoteDMATransfer(dst_ids=[to(x) for x in away], dma_engine_mask=0x00FF, remote_sem=S.b2,
+                                 srcs=[T.bc[:]], dsts=[T.bc[:] for x in away], alu_op=0)]
         if here:
-            trs.append(RemoteDMATransfer(dst_ids=[to(here[0])], dma_engine_mask=0xFF00, remote_sem=S.b2,
-                                         src=T.bc[:], dst=T.bc[:]))
+            trs.append(tr(here[0], 0xFF00, S.b2, [T.bc[:]], T.bc[:]))
         g.remote_dma_fused(trs, local_sem=S.sent)
         g.wait_ge(S.sent, 8 * len(trs))

@@ -16,7 +16,6 @@ SCRATCH = {
 SEMAPHORES = ["ld1", "ld2", "st", "st2", "w1", "w2", "a1", "a2", "a3", "b1", "b2", "sent"]
 
 X_CORE, M_CORE, B_CORE = 2, 7, 6
-BC_FIRST = True
 
 
 def cid(h, p, k):
@@ -45,51 +44,47 @@ def rank_program(g, core, T, topo):
     rh, rp = root // 128, (root % 128) // 8
     far = cid(3 - rh, rp, B_CORE)
     near = cid(rh, rp, B_CORE)
+    xw = {x: (4 if x == root else 8) for x in T.cores}
 
     if k == 0:
-        def send_x2():
-            g.wait_ge(S.ld2, 16)
-            g.remote_dma_fused([tr(far, 0x00FF, S.b1, [T.bc[:]], T.bc[:]), tr(near, 0xFF00, S.b1, [T.bc[:]], T.bc[:])],
-                               local_sem=S.sent)
-
         is_root = core == root
-        if is_root and BC_FIRST:
-            g.dma_start(out=T.bc[:], in_=T.x2[:]).then_inc(S.ld2, 16)
         g.dma_start(out=T.xs[:], in_=T.x1[:]).then_inc(S.ld1, 16)
-        if is_root and not BC_FIRST:
+        if is_root:
             g.dma_start(out=T.bc[:], in_=T.x2[:]).then_inc(S.ld2, 16)
-        if is_root and BC_FIRST:
-            send_x2()
         g.wait_ge(S.ld1, 16)
-        g.remote_dma_fused([
-            tr(cid(s, p, X_CORE), 0x00FF, S.w1, [T.xs[:, 128 * (h ^ 2):128 * (h ^ 2) + 128]], T.inb[:]),
-            tr(cid(h, p, X_CORE), 0xFF00, S.w1, [T.xs[:, 128 * c:128 * c + 128]], T.ina[:]),
-        ], local_sem=S.sent)
-        if is_root and not BC_FIRST:
-            send_x2()
+        pd, pc = T.xs[:, 128 * (h ^ 2):128 * (h ^ 2) + 128], T.xs[:, 128 * c:128 * c + 128]
+        if is_root:
+            g.wait_ge(S.ld2, 16)
+            g.remote_dma_fused([
+                tr(cid(s, p, X_CORE), 0x000F, S.w1, [pd], T.inb[:]), tr(far, 0x00F0, S.b1, [T.bc[:]], T.bc[:]),
+                tr(cid(h, p, X_CORE), 0x0F00, S.w1, [pc], T.ina[:]), tr(near, 0xF000, S.b1, [T.bc[:]], T.bc[:]),
+            ], local_sem=S.sent)
+        else:
+            g.remote_dma_fused([tr(cid(s, p, X_CORE), 0x00FF, S.w1, [pd], T.inb[:]),
+                                tr(cid(h, p, X_CORE), 0xFF00, S.w1, [pc], T.ina[:])], local_sem=S.sent)
         g.remote_dma_fused([
             tr(cid(s, p, 0), 0x000F, S.a1, [blk(T.xs, 2 * s + p)], T.nb[:]),
             tr(cid(s, p, M_CORE), 0x00F0, S.w1, [blk(T.xs, 2 * s + q)], T.mb[:]),
             tr(cid(h, p, M_CORE), 0xFF00, S.w1, [blk(T.xs, 2 * h + q)], T.ma[:]),
         ], local_sem=S.sent)
         g.dma_start(out=T.y1[:], in_=blk(T.x1, 2 * h + p)).then_inc(S.st, 16)
+        if is_root:
+            g.dma_start(out=T.y2[:], in_=T.x2[:]).then_inc(S.st2, 16)
         n = 16
-        for sem, cnt, buf in ((S.a1, 4, T.nb), (S.a2, 8, T.n2), (S.a3, 8, T.fp)):
+        for i, (sem, cnt, buf) in enumerate(((S.a1, 4, T.nb), (S.a2, 8, T.n2), (S.a3, 8, T.fp))):
+            if i == 2 and not is_root:
+                g.wait_ge(S.b2, 8)
+                g.dma_start(out=T.y2[:], in_=T.bc[:]).then_inc(S.st2, 16)
             g.wait_ge(sem, cnt)
             g.wait_ge(S.st, n)
             g.dma_start(out=T.y1[:], in_=buf[:], accum_op=AluOpType.add, max_dma_last_dim=8192).then_inc(S.st, 16)
             n += 16
-        if is_root:
-            g.dma_start(out=T.y2[:], in_=T.x2[:]).then_inc(S.st2, 16)
-        else:
-            g.wait_ge(S.b2, 8)
-            g.dma_start(out=T.y2[:], in_=T.bc[:]).then_inc(S.st2, 16)
-        g.wait_ge(S.sent, 48 if is_root else 32)
+        g.wait_ge(S.sent, 32)
         g.wait_ge(S.st, n)
         g.wait_ge(S.st2, 16)
 
     elif k == X_CORE:
-        g.wait_ge(S.w1, 16)
+        g.wait_ge(S.w1, xw[cid(h, p, 0)] + xw[cid(s, p, 0)])
         g.remote_dma_fused([tr(cid(h, q, X_CORE), 0x00FF, S.w2, [blk(T.ina, q), blk(T.inb, q)], T.pm[:])], local_sem=S.sent)
         g.wait_ge(S.w2, 8)
         g.remote_dma_fused([tr(cid(c, p, 0), 0x00FF, S.a3, [blk(T.ina, p), blk(T.inb, p), T.pm[:]], T.fp[:])],
@@ -105,7 +100,7 @@ def rank_program(g, core, T, topo):
         rack = [x for x in T.cores if topo.rack(topo.host(x)) == topo.rack(h) and x != root]
         here = [x for x in rack if x // 8 == core // 8]
         away = [x for x in rack if x // 8 != core // 8]
-        g.wait_ge(S.b1, 8)
+        g.wait_ge(S.b1, 4)
         trs = [RemoteDMATransfer(dst_ids=[to(x) for x in away], dma_engine_mask=0x00FF, remote_sem=S.b2,
                                  srcs=[T.bc[:]], dsts=[T.bc[:] for x in away], alu_op=0)]
         if here:

@@ -11,7 +11,7 @@ SCRATCH = {
     "nb": ("dram", [128, 64], "float32"),
     "n2": ("dram", [128, 64], "float32"),
     "fp": ("dram", [128, 64], "float32"),
-    "bc": ("dram", [128, 128], "float32"),
+    "bc": ("dram", [2, 128, 64], "float32"),
 }
 SEMAPHORES = ["ld1", "ld2", "st", "st2", "w1", "w2", "a1", "a2", "a3", "b1", "b2", "sent"]
 
@@ -44,7 +44,9 @@ def rank_program(g, core, T, topo):
     rh, rp = root // 128, (root % 128) // 8
     far = cid(3 - rh, rp, B_CORE)
     near = cid(rh, rp, B_CORE)
-    xw = {x: (4 if x == root else 8) for x in T.cores}
+
+    def off_w(x):
+        return 2 if x == root else 4
 
     if k == 0:
         is_root = core == root
@@ -52,26 +54,29 @@ def rank_program(g, core, T, topo):
         if is_root:
             g.dma_start(out=T.bc[:], in_=T.x2[:]).then_inc(S.ld2, 16)
         g.wait_ge(S.ld1, 16)
-        pd, pc = T.xs[:, 128 * (h ^ 2):128 * (h ^ 2) + 128], T.xs[:, 128 * c:128 * c + 128]
+        g.remote_dma_fused([
+            tr(cid(s, p, X_CORE), 0x00FF, S.w1, [T.xs[:, 128 * (h ^ 2):128 * (h ^ 2) + 128]], T.inb[:]),
+            tr(cid(h, p, X_CORE), 0xFF00, S.w1, [T.xs[:, 128 * c:128 * c + 128]], T.ina[:]),
+        ], local_sem=S.sent)
+        b_nb, b_mb, b_ma = blk(T.xs, 2 * s + p), blk(T.xs, 2 * s + q), blk(T.xs, 2 * h + q)
         if is_root:
             g.wait_ge(S.ld2, 16)
             g.remote_dma_fused([
-                tr(cid(s, p, X_CORE), 0x000F, S.w1, [pd], T.inb[:]), tr(far, 0x00F0, S.b1, [T.bc[:]], T.bc[:]),
-                tr(cid(h, p, X_CORE), 0x0F00, S.w1, [pc], T.ina[:]), tr(near, 0xF000, S.b1, [T.bc[:]], T.bc[:]),
+                tr(cid(s, p, 0), 0x0003, S.a1, [b_nb], T.nb[:]), tr(cid(s, p, M_CORE), 0x000C, S.w1, [b_mb], T.mb[:]),
+                tr(far, 0x0030, S.b1, [T.bc[0]], T.bc[0]), tr(far, 0x00C0, S.b1, [T.bc[1]], T.bc[1]),
+                tr(cid(h, p, M_CORE), 0x0F00, S.w1, [b_ma], T.ma[:]),
+                tr(near, 0x3000, S.b1, [T.bc[0]], T.bc[0]), tr(near, 0xC000, S.b1, [T.bc[1]], T.bc[1]),
             ], local_sem=S.sent)
         else:
-            g.remote_dma_fused([tr(cid(s, p, X_CORE), 0x00FF, S.w1, [pd], T.inb[:]),
-                                tr(cid(h, p, X_CORE), 0xFF00, S.w1, [pc], T.ina[:])], local_sem=S.sent)
-        g.remote_dma_fused([
-            tr(cid(s, p, 0), 0x000F, S.a1, [blk(T.xs, 2 * s + p)], T.nb[:]),
-            tr(cid(s, p, M_CORE), 0x00F0, S.w1, [blk(T.xs, 2 * s + q)], T.mb[:]),
-            tr(cid(h, p, M_CORE), 0xFF00, S.w1, [blk(T.xs, 2 * h + q)], T.ma[:]),
-        ], local_sem=S.sent)
+            g.remote_dma_fused([
+                tr(cid(s, p, 0), 0x000F, S.a1, [b_nb], T.nb[:]), tr(cid(s, p, M_CORE), 0x00F0, S.w1, [b_mb], T.mb[:]),
+                tr(cid(h, p, M_CORE), 0xFF00, S.w1, [b_ma], T.ma[:]),
+            ], local_sem=S.sent)
         g.dma_start(out=T.y1[:], in_=blk(T.x1, 2 * h + p)).then_inc(S.st, 16)
         if is_root:
             g.dma_start(out=T.y2[:], in_=T.x2[:]).then_inc(S.st2, 16)
         n = 16
-        for i, (sem, cnt, buf) in enumerate(((S.a1, 4, T.nb), (S.a2, 8, T.n2), (S.a3, 8, T.fp))):
+        for i, (sem, cnt, buf) in enumerate(((S.a1, off_w(cid(s, p, 0)), T.nb), (S.a2, 8, T.n2), (S.a3, 8, T.fp))):
             if i == 2 and not is_root:
                 g.wait_ge(S.b2, 8)
                 g.dma_start(out=T.y2[:], in_=T.bc[:]).then_inc(S.st2, 16)
@@ -84,7 +89,7 @@ def rank_program(g, core, T, topo):
         g.wait_ge(S.st2, 16)
 
     elif k == X_CORE:
-        g.wait_ge(S.w1, xw[cid(h, p, 0)] + xw[cid(s, p, 0)])
+        g.wait_ge(S.w1, 16)
         g.remote_dma_fused([tr(cid(h, q, X_CORE), 0x00FF, S.w2, [blk(T.ina, q), blk(T.inb, q)], T.pm[:])], local_sem=S.sent)
         g.wait_ge(S.w2, 8)
         g.remote_dma_fused([tr(cid(c, p, 0), 0x00FF, S.a3, [blk(T.ina, p), blk(T.inb, p), T.pm[:]], T.fp[:])],
@@ -92,7 +97,7 @@ def rank_program(g, core, T, topo):
         g.wait_ge(S.sent, 16)
 
     elif k == M_CORE:
-        g.wait_ge(S.w1, 12)
+        g.wait_ge(S.w1, 2 * off_w(cid(h, p, 0)) + off_w(cid(s, p, 0)))
         g.remote_dma_fused([tr(cid(h, q, 0), 0x00FF, S.a2, [T.ma[:], T.mb[:]], T.n2[:])], local_sem=S.sent)
         g.wait_ge(S.sent, 8)
 
@@ -101,9 +106,11 @@ def rank_program(g, core, T, topo):
         here = [x for x in rack if x // 8 == core // 8]
         away = [x for x in rack if x // 8 != core // 8]
         g.wait_ge(S.b1, 4)
-        trs = [RemoteDMATransfer(dst_ids=[to(x) for x in away], dma_engine_mask=0x00FF, remote_sem=S.b2,
-                                 srcs=[T.bc[:]], dsts=[T.bc[:] for x in away], alu_op=0)]
-        if here:
-            trs.append(tr(here[0], 0xFF00, S.b2, [T.bc[:]], T.bc[:]))
+        trs = []
+        for i in range(2):
+            trs.append(RemoteDMATransfer(dst_ids=[to(x) for x in away], dma_engine_mask=0x000F << (4 * i), remote_sem=S.b2,
+                                         srcs=[T.bc[i]], dsts=[T.bc[i] for x in away], alu_op=0))
+            if here:
+                trs.append(tr(here[0], 0x0F00 << (4 * i), S.b2, [T.bc[i]], T.bc[i]))
         g.remote_dma_fused(trs, local_sem=S.sent)
-        g.wait_ge(S.sent, 8 * len(trs))
+        g.wait_ge(S.sent, 4 * len(trs))

@@ -15,7 +15,8 @@ SCRATCH = {
 }
 SEMAPHORES = ["ld1", "ld2", "st", "st2", "w1", "w2", "a1", "a2", "a3", "b1", "b2", "sent"]
 
-X_CORE, M_CORE, B_CORE = 2, 7, 6
+X_CORE, M_CORE = 2, 7
+B_CORES = (6, 3)
 
 
 def cid(h, p, k):
@@ -42,8 +43,8 @@ def rank_program(g, core, T, topo):
 
     root = T.cores[6]
     rh, rp = root // 128, (root % 128) // 8
-    far = cid(3 - rh, rp, B_CORE)
-    near = cid(rh, rp, B_CORE)
+    far = [cid(3 - rh, rp, b) for b in B_CORES]
+    near = [cid(rh, rp, b) for b in B_CORES]
 
     def off_w(x):
         return 2 if x == root else 4
@@ -63,9 +64,9 @@ def rank_program(g, core, T, topo):
             g.wait_ge(S.ld2, 16)
             g.remote_dma_fused([
                 tr(cid(s, p, 0), 0x0003, S.a1, [b_nb], T.nb[:]), tr(cid(s, p, M_CORE), 0x000C, S.w1, [b_mb], T.mb[:]),
-                tr(far, 0x0030, S.b1, [T.bc[0]], T.bc[0]), tr(far, 0x00C0, S.b1, [T.bc[1]], T.bc[1]),
+                tr(far[0], 0x0030, S.b1, [T.bc[0]], T.bc[0]), tr(far[1], 0x00C0, S.b1, [T.bc[1]], T.bc[1]),
                 tr(cid(h, p, M_CORE), 0x0F00, S.w1, [b_ma], T.ma[:]),
-                tr(near, 0x3000, S.b1, [T.bc[0]], T.bc[0]), tr(near, 0xC000, S.b1, [T.bc[1]], T.bc[1]),
+                tr(near[0], 0x3000, S.b1, [T.bc[0]], T.bc[0]), tr(near[1], 0xC000, S.b1, [T.bc[1]], T.bc[1]),
             ], local_sem=S.sent)
         else:
             g.remote_dma_fused([
@@ -78,7 +79,7 @@ def rank_program(g, core, T, topo):
         n = 16
         for i, (sem, cnt, buf) in enumerate(((S.a1, off_w(cid(s, p, 0)), T.nb), (S.a2, 8, T.n2), (S.a3, 8, T.fp))):
             if i == 2 and not is_root:
-                g.wait_ge(S.b2, 8)
+                g.wait_ge(S.b2, 16)
                 g.dma_start(out=T.y2[:], in_=T.bc[:]).then_inc(S.st2, 16)
             g.wait_ge(sem, cnt)
             g.wait_ge(S.st, n)
@@ -101,16 +102,15 @@ def rank_program(g, core, T, topo):
         g.remote_dma_fused([tr(cid(h, q, 0), 0x00FF, S.a2, [T.ma[:], T.mb[:]], T.n2[:])], local_sem=S.sent)
         g.wait_ge(S.sent, 8)
 
-    elif core in (far, near):
+    elif core in far or core in near:
+        i = B_CORES.index(k)
         rack = [x for x in T.cores if topo.rack(topo.host(x)) == topo.rack(h) and x != root]
         here = [x for x in rack if x // 8 == core // 8]
         away = [x for x in rack if x // 8 != core // 8]
-        g.wait_ge(S.b1, 4)
-        trs = []
-        for i in range(2):
-            trs.append(RemoteDMATransfer(dst_ids=[to(x) for x in away], dma_engine_mask=0x000F << (4 * i), remote_sem=S.b2,
-                                         srcs=[T.bc[i]], dsts=[T.bc[i] for x in away], alu_op=0))
-            if here:
-                trs.append(tr(here[0], 0x0F00 << (4 * i), S.b2, [T.bc[i]], T.bc[i]))
+        g.wait_ge(S.b1, 2)
+        trs = [RemoteDMATransfer(dst_ids=[to(x) for x in away], dma_engine_mask=0x00FF, remote_sem=S.b2,
+                                 srcs=[T.bc[i]], dsts=[T.bc[i] for x in away], alu_op=0)]
+        if here:
+            trs.append(tr(here[0], 0xFF00, S.b2, [T.bc[i]], T.bc[i]))
         g.remote_dma_fused(trs, local_sem=S.sent)
-        g.wait_ge(S.sent, 4 * len(trs))
+        g.wait_ge(S.sent, 8 * len(trs))

@@ -76,15 +76,22 @@ def rank_program(g, core, T, topo):
         g.dma_start(out=T.y1[:], in_=blk(T.x1, 2 * h + p)).then_inc(S.st, 16)
         if is_root:
             g.dma_start(out=T.y2[:], in_=T.x2[:]).then_inc(S.st2, 16)
+
+        def store_y2():
+            g.wait_ge(S.b2, 16)
+            g.dma_start(out=T.y2[:], in_=T.bc[:]).then_inc(S.st2, 16)
+
+        same_rack = topo.rack(h) == topo.rack(rh)
         n = 16
         for i, (sem, cnt, buf) in enumerate(((S.a1, off_w(cid(s, p, 0)), T.nb), (S.a2, 8, T.n2), (S.a3, 8, T.fp))):
-            if i == 2 and not is_root:
-                g.wait_ge(S.b2, 16)
-                g.dma_start(out=T.y2[:], in_=T.bc[:]).then_inc(S.st2, 16)
+            if i == 2 and same_rack and not is_root:
+                store_y2()
             g.wait_ge(sem, cnt)
             g.wait_ge(S.st, n)
             g.dma_start(out=T.y1[:], in_=buf[:], accum_op=AluOpType.add, max_dma_last_dim=8192).then_inc(S.st, 16)
             n += 16
+        if not same_rack:
+            store_y2()
         g.wait_ge(S.sent, 32)
         g.wait_ge(S.st, n)
         g.wait_ge(S.st2, 16)

from concourse.bass import DstId, RemoteDMATransfer
from concourse.mybir import AluOpType

SCRATCH = {
    "xs": ("sbuf", [128, 512], "float32"),
    "ina": ("sbuf", [128, 128], "float32"),
    "inb": ("sbuf", [128, 128], "float32"),
    "pm": ("sbuf", [128, 64], "float32"),
    "ma": ("sbuf", [128, 64], "float32"),
    "mb": ("sbuf", [128, 64], "float32"),
    "nb": ("dram", [128, 64], "float32"),
    "n2": ("dram", [128, 64], "float32"),
    "fp": ("dram", [128, 64], "float32"),
    "bc": ("dram", [2, 128, 64], "float32"),
}
SEMAPHORES = ["ld1", "ld2", "st", "st2", "w1", "w2", "a1", "a2", "a3", "b1", "b2", "sent"]

X_CORE, M_CORE = 2, 7
B_CORES = (6, 3)


def cid(h, p, k):
    return 128 * h + 8 * p + k


def rank_program(g, core, T, topo):
    h, p, k = core // 128, (core % 128) // 8, core % 8
    if p > 1:
        return
    S = T.sem
    s, c, q = h ^ 1, 3 - h, 1 - p

    def to(d):
        rid, pid = topo.addr(d, core)
        return DstId(rid=rid, pnc=pid)

    def blk(t, b):
        return t[:, 64 * b:64 * b + 64]

    def tr(d, mask, sem, srcs, dst):
        return RemoteDMATransfer(dst_ids=[to(d)], dma_engine_mask=mask, remote_sem=sem, srcs=srcs, dsts=[dst],
                                 alu_op=1 if len(srcs) > 1 else 0)

    root = T.cores[6]
    rh, rp = root // 128, (root % 128) // 8
    far = [cid(3 - rh, rp, b) for b in B_CORES]
    near = [cid(rh, rp, b) for b in B_CORES]

    def off_w(x):
        return 2 if x == root else 4

    if k == 0:
        is_root = core == root
        g.dma_start(out=T.xs[:], in_=T.x1[:]).then_inc(S.ld1, 16)
        if is_root:
            g.dma_start(out=T.bc[:], in_=T.x2[:]).then_inc(S.ld2, 16)
        g.wait_ge(S.ld1, 16)
        g.remote_dma_fused([
            tr(cid(s, p, X_CORE), 0x00FF, S.w1, [T.xs[:, 128 * (h ^ 2):128 * (h ^ 2) + 128]], T.inb[:]),
            tr(cid(h, p, X_CORE), 0xFF00, S.w1, [T.xs[:, 128 * c:128 * c + 128]], T.ina[:]),
        ], local_sem=S.sent)
        b_nb, b_mb, b_ma = blk(T.xs, 2 * s + p), blk(T.xs, 2 * s + q), blk(T.xs, 2 * h + q)
        if is_root:
            g.wait_ge(S.ld2, 16)
            g.remote_dma_fused([
                tr(cid(s, p, 0), 0x0003, S.a1, [b_nb], T.nb[:]), tr(cid(s, p, M_CORE), 0x000C, S.w1, [b_mb], T.mb[:]),
                tr(far[0], 0x0030, S.b1, [T.bc[0]], T.bc[0]), tr(far[1], 0x00C0, S.b1, [T.bc[1]], T.bc[1]),
                tr(cid(h, p, M_CORE), 0x0F00, S.w1, [b_ma], T.ma[:]),
                tr(near[0], 0x3000, S.b1, [T.bc[0]], T.bc[0]), tr(near[1], 0xC000, S.b1, [T.bc[1]], T.bc[1]),
            ], local_sem=S.sent)
        else:
            g.remote_dma_fused([
                tr(cid(s, p, 0), 0x000F, S.a1, [b_nb], T.nb[:]), tr(cid(s, p, M_CORE), 0x00F0, S.w1, [b_mb], T.mb[:]),
                tr(cid(h, p, M_CORE), 0xFF00, S.w1, [b_ma], T.ma[:]),
            ], local_sem=S.sent)
        g.dma_start(out=T.y1[:], in_=blk(T.x1, 2 * h + p)).then_inc(S.st, 16)
        if is_root:
            g.dma_start(out=T.y2[:], in_=T.x2[:]).then_inc(S.st2, 16)

        def store_y2():
            g.wait_ge(S.b2, 16)
            g.dma_start(out=T.y2[:], in_=T.bc[:]).then_inc(S.st2, 16)

        same_rack = topo.rack(h) == topo.rack(rh)
        n = 16
        for i, (sem, cnt, buf) in enumerate(((S.a1, off_w(cid(s, p, 0)), T.nb), (S.a2, 8, T.n2), (S.a3, 8, T.fp))):
            if i == 2 and same_rack and not is_root:
                store_y2()
            g.wait_ge(sem, cnt)
            g.wait_ge(S.st, n)
            g.dma_start(out=T.y1[:], in_=buf[:], accum_op=AluOpType.add, max_dma_last_dim=8192).then_inc(S.st, 16)
            n += 16
        if not same_rack:
            store_y2()
        g.wait_ge(S.sent, 32)
        g.wait_ge(S.st, n)
        g.wait_ge(S.st2, 16)

    elif k == X_CORE:
        g.wait_ge(S.w1, 16)
        g.remote_dma_fused([tr(cid(h, q, X_CORE), 0x00FF, S.w2, [blk(T.ina, q), blk(T.inb, q)], T.pm[:])], local_sem=S.sent)
        g.wait_ge(S.w2, 8)
        g.remote_dma_fused([tr(cid(c, p, 0), 0x00FF, S.a3, [blk(T.ina, p), blk(T.inb, p), T.pm[:]], T.fp[:])],
                           local_sem=S.sent)
        g.wait_ge(S.sent, 16)

    elif k == M_CORE:
        g.wait_ge(S.w1, 2 * off_w(cid(h, p, 0)) + off_w(cid(s, p, 0)))
        g.remote_dma_fused([tr(cid(h, q, 0), 0x00FF, S.a2, [T.ma[:], T.mb[:]], T.n2[:])], local_sem=S.sent)
        g.wait_ge(S.sent, 8)

    elif core in far or core in near:
        i = B_CORES.index(k)
        rack = [x for x in T.cores if topo.rack(topo.host(x)) == topo.rack(h) and x != root]
        here = [x for x in rack if x // 8 == core // 8]
        away = [x for x in rack if x // 8 != core // 8]
        g.wait_ge(S.b1, 2)
        trs = [RemoteDMATransfer(dst_ids=[to(x) for x in away], dma_engine_mask=0x00FF, remote_sem=S.b2,
                                 srcs=[T.bc[i]], dsts=[T.bc[i] for x in away], alu_op=0)]
        if here:
            trs.append(tr(here[0], 0xFF00, S.b2, [T.bc[i]], T.bc[i]))
        g.remote_dma_fused(trs, local_sem=S.sent)
        g.wait_ge(S.sent, 8 * len(trs))
